import numpy as np
import ml_dtypes


def mxq(x, axis, fmt="e4m3"):
    dtype, down = {"e4m3": (ml_dtypes.float8_e4m3fn, 7), "e5m2": (ml_dtypes.float8_e5m2, 14)}[fmt]
    v = np.moveaxis(np.asarray(x, np.float32).astype(ml_dtypes.bfloat16).astype(np.float64), axis, -1)
    blocks = v.reshape(v.shape[:-1] + (-1, 32))
    amax = np.abs(blocks).max(-1, keepdims=True)
    byte = np.maximum(np.where(amax > 0, np.frexp(amax)[1] - 1 + 127, 0) - down, 1)
    scale = np.exp2(byte - 127.0)
    codes = (blocks / scale).astype(np.float32).astype(dtype).astype(np.float64)
    return np.moveaxis((codes * scale).reshape(v.shape), -1, axis)


WIDE = False


def mx_kscale(k):
    if not WIDE:
        return np.ones(k)
    levels = np.array([10, -10, 5, -5, 0])
    if k % 512:
        return np.exp2(np.random.permutation(np.resize(levels, k // 32))).repeat(32)
    a = np.empty((k // 512, 16))
    for p in range(k // 512):
        a[p, :8] = np.random.permutation(np.resize(levels, 8))
        for g in range(8):
            far = levels[np.abs(levels - a[p, g]) >= 10]
            a[p, g + 8] = far[np.random.randint(len(far))]
    return np.exp2(a.ravel()).repeat(32)


BF16 = ml_dtypes.bfloat16


def bf(x):
    return np.asarray(x, np.float32).astype(BF16)


def f64(x):
    return np.asarray(x).astype(np.float64)


E2M1 = np.array([0.0, 0.5, 1.0, 1.5, 2.0, 3.0, 4.0, 6.0, -0.0, -0.5, -1.0, -1.5, -2.0, -3.0, -4.0, -6.0])


def pack_weight(w, fmt):
    k, n = w.shape
    w = f64(bf(w)).reshape(k // 32, 32, n)
    amax = np.abs(w).max(1)
    if fmt == "e4m3":
        byte = np.frexp(amax)[1] - 1 + 127 - 7
    else:
        mant, ex = np.frexp(amax / 6.0)
        byte = np.where(mant > 0.5, ex, ex - 1) + 127
    byte = np.clip(np.where(amax > 0, byte, 1), 1, 254)
    scaled = (w * np.exp2(127.0 - byte)[:, None, :]).reshape(k, n).astype(np.float32)
    by_word = np.ascontiguousarray(scaled.reshape(k // 512, 128, 4, n).transpose(0, 1, 3, 2))
    if fmt == "e4m3":
        words = by_word.astype(ml_dtypes.float8_e4m3fn).view(np.uint8)
    else:
        c = by_word.astype(ml_dtypes.float4_e2m1fn).view(np.uint8) & 0xF
        words = c[..., 0::2] | (c[..., 1::2] << 4)
    return np.ascontiguousarray(words), np.ascontiguousarray(byte.astype(np.uint8).reshape(k // 512, 16, n))


def unpack_weight(words, scales, fmt):
    g, p, n, _ = words.shape
    if fmt == "e4m3":
        vals = np.ascontiguousarray(words).view(ml_dtypes.float8_e4m3fn).astype(np.float64)
    else:
        nib = np.empty((g, p, n, 4), np.uint8)
        nib[..., 0::2] = words & 0xF
        nib[..., 1::2] = words >> 4
        vals = E2M1[nib]
    vals = vals * np.repeat(np.exp2(scales.astype(np.float64) - 127.0), 8, axis=1)[..., None]
    return vals.transpose(0, 1, 3, 2).reshape(g * 512, n)
def pack4(w):
    words, scales = pack_weight(w, "e2m1")
    return words.reshape(words.shape[0], 128, -1), scales


def unpack4(words, scales):
    return unpack_weight(words.reshape(words.shape[0], 128, -1, 2), scales, "e2m1")


M, K, R, N = 1024, 2048, 512, 1536


def setup_inputs():
    s, v, t = mx_kscale(K), mx_kscale(K), mx_kscale(R)
    c = np.random.standard_normal((K, M)) * s[:, None]
    f = np.random.standard_normal((K, R)) / np.sqrt(K) / R ** 0.25 / s[:, None] * t
    c_words, c_scales = pack4(c)
    f_words, f_scales = pack4(f)
    return {"c_words": c_words, "c_scales": c_scales,
            "f_words": f_words, "f_scales": f_scales,
            "h": bf(np.random.standard_normal((R, K)) / np.sqrt(K) / R ** 0.25 / v / t[:, None]),
            "b": bf(np.random.standard_normal((K, N)) * v[:, None]),
            "d": bf(np.random.uniform(0.5, 1.5, R)),
            "r": bf(1 + 0.1 * np.random.standard_normal(M)),
            "a": bf(np.random.standard_normal((M, N)))}


def reference(c_words, c_scales, f_words, f_scales, h, b, d, r, a):
    c = unpack4(c_words, c_scales)
    f = unpack4(f_words, f_scales)
    lo = c.T @ f
    lo = lo * f64(r)[:, None]
    up = mxq(f64(h), 1, "e4m3") @ mxq(f64(b), 0, "e4m3")
    up = up * f64(d)[:, None]
    prod = mxq(lo, 1, "e4m3") @ mxq(up, 0, "e4m3")
    return f64(a) - prod

@@ -1,0 +1,333 @@
+from contextlib import ExitStack
+
+import concourse.mybir as mybir
+from concourse.masks import make_identity
+
+M, K, R, N = 1024, 2048, 512, 1536
+FLOPS = 2 * M * K * R + 2 * R * K * N + 2 * M * R * N
+
+F32 = mybir.dt.float32
+BF16 = mybir.dt.bfloat16
+I32 = mybir.dt.int32
+U32 = mybir.dt.uint32
+U8 = mybir.dt.uint8
+FP8X4 = mybir.dt.float8_e4m3fn_x4
+FP4X4 = mybir.dt.float4_e2m1fn_x4
+COPY = mybir.ActivationFunctionType.Copy
+SUBTRACT = mybir.AluOpType.subtract
+
+P = 128
+PACK = 4
+PASSES = K // (P * PACK)
+WIDE = 512
+CHUNKS = N // WIDE
+M_TILES = M // P
+PAIRS = M_TILES // 2
+STAGE_BUFS = 20
+
+
+def tile_row_scaled_schur_update_s12_kernel(tc, c_words, c_scales, f_words, f_scales, h, b, d, r, a, out):
+    nc = tc.nc
+    with ExitStack() as ctx:
+        sb = ctx.enter_context(tc.tile_pool(name="sb", bufs=1))
+        psum = ctx.enter_context(tc.psum_pool(name="psum", bufs=8))
+        ctx.enter_context(tc.manual_schedule())
+
+        def bank(name):
+            return psum.tile([P, WIDE], F32, name=name, tag="bank")
+
+        def stage(name, shape, dtype):
+            return sb.tile(shape, dtype, name=name, tag="stage", bufs=STAGE_BUFS, align_bytes=64)
+
+        def quantize(name, grouped):
+            words = grouped.shape[1] // PACK
+            codes = sb.tile([P, words], U32, name=name + "_codes", align_bytes=64)
+            scales = sb.tile([P, words], U8, name=name + "_scales", align_bytes=64)
+            nc.vector.quantize_mx(out=codes[:].bitcast(FP8X4), scales=scales[:], in_=grouped[:])
+            return codes, scales
+
+        def interleave(name, rows, vector_cols):
+            width = rows.shape[2]
+            grouped = sb.tile([P, PACK * width], BF16, name=name, tag="grouped", bufs=5, align_bytes=64)
+            dst = grouped[:].rearrange("p (c i t) -> p c t i", i=4, t=PACK)
+            src = rows[:].rearrange("p t (c i) -> p c t i", i=4)
+            cut = vector_cols // 4
+            if cut < width // 4:
+                nc.scalar.copy(out=dst[:, cut:], in_=src[:, cut:])
+            if cut > 0:
+                nc.vector.tensor_copy(out=dst[:, :cut], in_=src[:, :cut])
+            return grouped
+
+        c_plane = sb.tile([P, PASSES * M], U8, name="c_plane", align_bytes=64)
+        f_plane = sb.tile([P, PASSES * R], U8, name="f_plane", align_bytes=64)
+        nc.vector.memset(f_plane[:].bitcast(I32), 0)
+        nc.vector.memset(c_plane[:].bitcast(I32), 0)
+        d_raw = sb.tile([P, PACK], BF16, name="d_raw")
+        nc.gpsimd.dma_start(out=d_raw[:], in_=d.rearrange("(p t) -> p t", t=PACK))
+        r_rows = sb.tile([M_TILES, P], BF16, name="r_rows")
+        nc.gpsimd.dma_start(out=r_rows[:], in_=r.rearrange("(j p) -> j p", p=P))
+        ident = sb.tile([P, P], F32, name="ident")
+        make_identity(nc, ident[:])
+        r_square = sb.tile([P, P], F32, name="r_square")
+        nc.gpsimd.memset(r_square[:], 0.0)
+
+        def load_words(name, words, first, width):
+            tile = sb.tile([P, PASSES, width], U8, name=name, align_bytes=64)
+            src = words.rearrange("g p w -> p g w")[:, :, first : first + width]
+            nc.sync.dma_start(out=tile[:].bitcast(I32), in_=src.bitcast(I32))
+            return tile
+
+        def load_plane(plane, scales):
+            for row in range(4):
+                nc.sync.dma_start(
+                    out=plane[row:P:32, :].bitcast(I32).rearrange("q (g w) -> q g w", g=PASSES),
+                    in_=scales.bitcast(I32)[:, row:16:4, :].rearrange("g q w -> q g w"),
+                )
+
+        h_rows, b_rows, a_rows = {}, {}, {}
+
+        def load_h(t):
+            h_rows[t] = stage("h_rows%d" % t, [P, K], BF16)
+            nc.sync.dma_start(out=h_rows[t][:], in_=h.rearrange("(p t) k -> p t k", t=PACK)[:, t, :])
+
+        def load_b(chunk, g):
+            b_rows[chunk, g] = stage("b_rows%d_%d" % (chunk, g), [P, PACK, WIDE], BF16)
+            src = b[g * P * PACK : (g + 1) * P * PACK, chunk * WIDE : (chunk + 1) * WIDE]
+            nc.sync.dma_start(out=b_rows[chunk, g][:], in_=src.rearrange("(p t) n -> p t n", t=PACK))
+
+        def load_a(pair):
+            a_rows[pair] = sb.tile([P, 2, N], BF16, name="a_rows%d" % pair)
+            nc.sync.dma_start(out=a_rows[pair][:], in_=a.rearrange("(j p) n -> p j n", p=P)[:, 2 * pair : 2 * pair + 2, :])
+
+        c_tiles, f_tiles = {}, {}
+
+        def load_c(half):
+            c_tiles[half] = load_words("c_tile%d" % half, c_words, half * M, M)
+
+        def load_f():
+            f_tiles[0] = load_words("f_tile", f_words, 0, 2 * R)
+
+        def load_planes():
+            load_plane(f_plane, f_scales)
+            load_plane(c_plane, c_scales)
+
+        for s in range(PACK):
+            load_b(0, s)
+            load_h(s)
+        for g in range(PASSES):
+            load_b(1, g)
+        load_f()
+        load_c(0)
+        load_planes()
+        load_c(1)
+        for g in range(PASSES):
+            load_b(2, g)
+        for pair in range(PAIRS):
+            load_a(pair)
+
+        d_cols = sb.tile([P, PACK], F32, name="d_cols")
+        nc.scalar.activation(out=d_cols[:], in_=d_raw[:], func=COPY)
+        nc.vector.tensor_copy(out=r_square[0:M_TILES, :], in_=r_rows[:])
+        r_bank = bank("r_bank")
+        nc.tensor.transpose(out=r_bank[:, 0:P], in_=r_square[:], identity=ident[:])
+        r_cols = sb.tile([P, M_TILES], F32, name="r_cols")
+        nc.scalar.copy(out=r_cols[:], in_=r_bank[:, 0:M_TILES])
+
+        b_grouped, b_mx, h_grouped, h_mx, l_sorted, l_grouped, l_mx = {}, {}, {}, {}, {}, {}, {}
+        u_acc, u_rows, u_grouped, u_mx = {}, {}, {}, {}
+
+        def group_b(chunk, g, vector_cols):
+            b_grouped[chunk, g] = interleave("b_grouped%d_%d" % (chunk, g), b_rows[chunk, g], vector_cols)
+
+        def quant_b(chunk, g):
+            b_mx[chunk, g] = quantize("b%d_%d" % (chunk, g), b_grouped[chunk, g])
+
+        def turn_h(t):
+            words = h_rows[t][:].bitcast(F32)
+            h_grouped[t] = sb.tile([P, K], BF16, name="h_grouped%d" % t, tag="grouped", bufs=5, align_bytes=64)
+            for half in range(2):
+                turned = bank("h_turned%d_%d" % (t, half))
+                for i in range(2):
+                    g = 2 * half + i
+                    for u in range(2):
+                        nc.tensor.transpose(
+                            out=turned[:, (2 * i + u) * P : (2 * i + u + 1) * P],
+                            in_=words[:, 256 * g + u : 256 * (g + 1) : 2],
+                            identity=ident[:],
+                        )
+                nc.scalar.copy(
+                    out=h_grouped[t][:].bitcast(F32)[:, half * WIDE : (half + 1) * WIDE].rearrange("p (i c u) -> p i c u", i=2, u=2),
+                    in_=turned[:].rearrange("p (i u c) -> p i c u", i=2, u=2),
+                )
+
+        def quant_h(t):
+            h_mx[t] = quantize("h%d" % t, h_grouped[t])
+
+        def mul_l(j):
+            acc = bank("l_acc%d" % j)
+            c_tile = c_tiles[j // 4]
+            first = (j % 4) * 2 * P
+            for g in range(PASSES):
+                nc.tensor.matmul_mx(
+                    out=acc[:],
+                    lhsT=c_tile[:, g, first : first + 2 * P].bitcast(FP4X4),
+                    lhsT_scale=c_plane[:, g * M + j * P : g * M + (j + 1) * P],
+                    rhs=f_tiles[0][:, g, :].bitcast(FP4X4),
+                    rhs_scale=f_plane[:, g * R : (g + 1) * R],
+                    start=(g == 0),
+                    stop=(g == PASSES - 1),
+                )
+            l_sorted[j] = sb.tile([P, R], BF16, name="l_sorted%d" % j, tag="l_sorted", bufs=4)
+            nc.scalar.activation(
+                out=l_sorted[j][:].rearrange("m (u p e) -> m u p e", u=2, e=2),
+                in_=acc[:].rearrange("m (p u e) -> m u p e", u=2, e=2),
+                func=COPY,
+                scale=r_cols[:, j : j + 1],
+            )
+
+        def turn_l(pair):
+            turned = bank("l_turned%d" % pair)
+            for i in range(2):
+                words = l_sorted[2 * pair + i][:].bitcast(F32)
+                for u in range(2):
+                    nc.tensor.transpose(
+                        out=turned[:, (2 * i + u) * P : (2 * i + u + 1) * P],
+                        in_=words[:, u * P : (u + 1) * P],
+                        identity=ident[:],
+                    )
+            l_grouped[pair] = sb.tile([P, 2 * P * PACK], BF16, name="l_grouped%d" % pair, tag="l_grouped", bufs=2, align_bytes=64)
+            nc.scalar.copy(
+                out=l_grouped[pair][:].bitcast(F32).rearrange("p (i c u) -> p i c u", i=2, u=2),
+                in_=turned[:].rearrange("p (i u c) -> p i c u", i=2, u=2),
+            )
+
+        def quant_l(pair):
+            l_mx[pair] = quantize("l%d" % pair, l_grouped[pair])
+
+        def pass_u(first, width, t, g):
+            chunk, inside = divmod(first, WIDE)
+            if g == 0:
+                u_acc[first, t] = bank("u_acc%d_%d" % (first, t))
+            h_codes, h_scales = h_mx[t]
+            b_codes, b_scales = b_mx[chunk, g]
+            nc.tensor.matmul_mx(
+                out=u_acc[first, t][:, 0:width],
+                lhsT=h_codes[:, g * P : (g + 1) * P].bitcast(FP8X4),
+                lhsT_scale=h_scales[:, g * P : (g + 1) * P],
+                rhs=b_codes[:, inside : inside + width].bitcast(FP8X4),
+                rhs_scale=b_scales[:, inside : inside + width],
+                start=(g == 0),
+                stop=(g == PASSES - 1),
+            )
+            if g == PASSES - 1:
+                if t == 0:
+                    u_rows[first] = stage("u_rows%d" % first, [P, PACK, width], BF16)
+                nc.scalar.activation(out=u_rows[first][:, t, :], in_=u_acc[first, t][:, 0:width], func=COPY, scale=d_cols[:, t : t + 1])
+
+        def mul_u(first, width, t):
+            for g in range(PASSES):
+                pass_u(first, width, t, g)
+
+        def group_u(first, vector_cols):
+            u_grouped[first] = interleave("u_grouped%d" % first, u_rows[first], vector_cols)
+
+        def quant_u(first):
+            u_mx[first] = quantize("u%d" % first, u_grouped[first])
+
+        def finish(first, pair):
+            l_codes, l_scales = l_mx[pair]
+            u_codes, u_scales = u_mx[first]
+            width = u_codes.shape[1]
+            cols = slice(first, first + width)
+            per_bank = WIDE // width
+            result = stage("result%d_%d" % (first, pair), [P, 2, width], F32)
+            for i0 in range(0, 2, per_bank):
+                acc = bank("prod%d_%d_%d" % (first, pair, i0))
+                for i in range(i0, i0 + per_bank):
+                    nc.tensor.matmul_mx(
+                        out=acc[:, (i - i0) * width : (i - i0 + 1) * width],
+                        lhsT=l_codes[:, i * P : (i + 1) * P].bitcast(FP8X4),
+                        lhsT_scale=l_scales[:, i * P : (i + 1) * P],
+                        rhs=u_codes[:].bitcast(FP8X4),
+                        rhs_scale=u_scales[:],
+                        start=True,
+                        stop=True,
+                    )
+                nc.vector.tensor_tensor(
+                    out=result[:, i0 : i0 + per_bank, :],
+                    in0=a_rows[pair][:, i0 : i0 + per_bank, cols],
+                    in1=acc[:].rearrange("p (i n) -> p i n", i=per_bank),
+                    op=SUBTRACT,
+                )
+            nc.sync.dma_start(out=out.rearrange("(j p) n -> p j n", p=P)[:, 2 * pair : 2 * pair + 2, cols], in_=result[:])
+
+        group_b(0, 0, 512)
+        turn_h(0)
+        quant_b(0, 0)
+        for s in range(PACK):
+            if s < 3:
+                group_b(0, s + 1, 256)
+                quant_h(s)
+                turn_h(s + 1)
+                quant_b(0, s + 1)
+            else:
+                group_b(1, 0, 512)
+                quant_h(s)
+                quant_b(1, 0)
+                group_b(1, 1, 512)
+            for t in range(s):
+                pass_u(0, 512, t, s)
+            for g in range(s + 1):
+                pass_u(0, 512, s, g)
+        quant_b(1, 1)
+        group_b(1, 2, 256)
+        group_b(1, 3, 256)
+        quant_b(1, 2)
+        quant_b(1, 3)
+        for g in range(PASSES):
+            for t in range(PACK):
+                pass_u(512, 512, t, g)
+        group_u(0, 512)
+        mul_l(0)
+        quant_u(0)
+        group_u(512, 512)
+        mul_l(1)
+        group_b(2, 0, 512)
+        quant_u(512)
+        mul_l(2)
+        turn_l(0)
+        group_b(2, 1, 512)
+        quant_b(2, 0)
+        mul_l(3)
+        group_b(2, 2, 384)
+        quant_b(2, 1)
+        mul_l(4)
+        turn_l(1)
+        quant_l(0)
+        group_b(2, 3, 384)
+        quant_b(2, 2)
+        mul_l(5)
+        quant_b(2, 3)
+        quant_l(1)
+        mul_l(6)
+        turn_l(2)
+        finish(0, 0)
+        mul_l(7)
+        quant_l(2)
+        mul_u(1024, 512, 0)
+        turn_l(3)
+        finish(512, 0)
+        mul_u(1024, 512, 1)
+        mul_u(1024, 512, 2)
+        finish(0, 1)
+        quant_l(3)
+        mul_u(1024, 512, 3)
+        group_u(1024, 0)
+        finish(512, 1)
+        finish(0, 2)
+        finish(512, 2)
+        quant_u(1024)
+        finish(0, 3)
+        finish(512, 3)
+        for pair in range(PAIRS):
+            finish(1024, pair)

@@ -63,9 +63,9 @@ def tile_row_scaled_schur_update_s12_kernel(tc, c_words, c_scales, f_words, f_sc
         nc.vector.memset(f_plane[:].bitcast(I32), 0)
         nc.vector.memset(c_plane[:].bitcast(I32), 0)
         d_raw = sb.tile([P, PACK], BF16, name="d_raw")
-        nc.gpsimd.dma_start(out=d_raw[:], in_=d.rearrange("(p t) -> p t", t=PACK))
+        nc.scalar.dma_start(out=d_raw[:], in_=d.rearrange("(p t) -> p t", t=PACK))
         r_rows = sb.tile([M_TILES, P], BF16, name="r_rows")
-        nc.gpsimd.dma_start(out=r_rows[:], in_=r.rearrange("(j p) -> j p", p=P))
+        nc.scalar.dma_start(out=r_rows[:], in_=r.rearrange("(j p) -> j p", p=P))
         ident = sb.tile([P, P], F32, name="ident")
         make_identity(nc, ident[:])
         r_square = sb.tile([P, P], F32, name="r_square")
@@ -119,15 +119,17 @@ def tile_row_scaled_schur_update_s12_kernel(tc, c_words, c_scales, f_words, f_sc
         load_f()
         load_c(0)
         load_planes()
+        load_b(2, 0)
+        load_b(2, 1)
         load_c(1)
-        for g in range(PASSES):
-            load_b(2, g)
+        load_b(2, 2)
+        load_b(2, 3)
         for pair in range(PAIRS):
             load_a(pair)
 
         d_cols = sb.tile([P, PACK], F32, name="d_cols")
         nc.scalar.activation(out=d_cols[:], in_=d_raw[:], func=COPY)
-        nc.vector.tensor_copy(out=r_square[0:M_TILES, :], in_=r_rows[:])
+        nc.scalar.copy(out=r_square[0:M_TILES, :], in_=r_rows[:])
         r_bank = bank("r_bank")
         nc.tensor.transpose(out=r_bank[:, 0:P], in_=r_square[:], identity=ident[:])
         r_cols = sb.tile([P, M_TILES], F32, name="r_cols")
@@ -234,20 +236,22 @@ def tile_row_scaled_schur_update_s12_kernel(tc, c_words, c_scales, f_words, f_sc
         def quant_u(first):
             u_mx[first] = quantize("u%d" % first, u_grouped[first])
 
-        def finish(first, pair):
-            l_codes, l_scales = l_mx[pair]
+        def finish(first, tile0):
             u_codes, u_scales = u_mx[first]
             width = u_codes.shape[1]
             cols = slice(first, first + width)
             per_bank = WIDE // width
-            result = stage("result%d_%d" % (first, pair), [P, 2, width], F32)
-            for i0 in range(0, 2, per_bank):
-                acc = bank("prod%d_%d_%d" % (first, pair, i0))
-                for i in range(i0, i0 + per_bank):
+            result = stage("result%d_%d" % (first, tile0), [P, 2 * per_bank, width], F32)
+            for i0 in range(0, 2 * per_bank, per_bank):
+                pair, inside = divmod(tile0 + i0, 2)
+                l_codes, l_scales = l_mx[pair]
+                acc = bank("prod%d_%d" % (first, tile0 + i0))
+                for i in range(per_bank):
+                    rows = slice((inside + i) * P, (inside + i + 1) * P)
                     nc.tensor.matmul_mx(
-                        out=acc[:, (i - i0) * width : (i - i0 + 1) * width],
-                        lhsT=l_codes[:, i * P : (i + 1) * P].bitcast(FP8X4),
-                        lhsT_scale=l_scales[:, i * P : (i + 1) * P],
+                        out=acc[:, i * width : (i + 1) * width],
+                        lhsT=l_codes[:, rows].bitcast(FP8X4),
+                        lhsT_scale=l_scales[:, rows],
                         rhs=u_codes[:].bitcast(FP8X4),
                         rhs_scale=u_scales[:],
                         start=True,
@@ -255,79 +259,87 @@ def tile_row_scaled_schur_update_s12_kernel(tc, c_words, c_scales, f_words, f_sc
                     )
                 nc.vector.tensor_tensor(
                     out=result[:, i0 : i0 + per_bank, :],
-                    in0=a_rows[pair][:, i0 : i0 + per_bank, cols],
+                    in0=a_rows[pair][:, inside : inside + per_bank, cols],
                     in1=acc[:].rearrange("p (i n) -> p i n", i=per_bank),
                     op=SUBTRACT,
                 )
-            nc.sync.dma_start(out=out.rearrange("(j p) n -> p j n", p=P)[:, 2 * pair : 2 * pair + 2, cols], in_=result[:])
+            nc.sync.dma_start(out=out.rearrange("(j p) n -> p j n", p=P)[:, tile0 : tile0 + 2 * per_bank, cols], in_=result[:])
 
-        group_b(0, 0, 512)
+        group_b(0, 0, 256)
         turn_h(0)
         quant_b(0, 0)
         for s in range(PACK):
             if s < 3:
-                group_b(0, s + 1, 256)
+                group_b(0, s + 1, 384)
                 quant_h(s)
                 turn_h(s + 1)
                 quant_b(0, s + 1)
             else:
                 group_b(1, 0, 512)
+                group_b(1, 1, 0)
                 quant_h(s)
                 quant_b(1, 0)
-                group_b(1, 1, 512)
+                group_b(1, 2, 512)
             for t in range(s):
                 pass_u(0, 512, t, s)
             for g in range(s + 1):
                 pass_u(0, 512, s, g)
         quant_b(1, 1)
-        group_b(1, 2, 256)
-        group_b(1, 3, 256)
         quant_b(1, 2)
+        group_b(1, 3, 512)
+        group_u(0, 0)
         quant_b(1, 3)
         for g in range(PASSES):
             for t in range(PACK):
                 pass_u(512, 512, t, g)
-        group_u(0, 512)
-        mul_l(0)
         quant_u(0)
-        group_u(512, 512)
-        mul_l(1)
         group_b(2, 0, 512)
-        quant_u(512)
-        mul_l(2)
-        turn_l(0)
+        mul_l(0)
+        mul_l(1)
         group_b(2, 1, 512)
         quant_b(2, 0)
+        mul_l(2)
+        turn_l(0)
+        group_u(512, 384)
+        quant_b(2, 1)
         mul_l(3)
         group_b(2, 2, 384)
-        quant_b(2, 1)
+        quant_u(512)
         mul_l(4)
         turn_l(1)
         quant_l(0)
         group_b(2, 3, 384)
         quant_b(2, 2)
         mul_l(5)
-        quant_b(2, 3)
-        quant_l(1)
-        mul_l(6)
-        turn_l(2)
         finish(0, 0)
-        mul_l(7)
-        quant_l(2)
-        mul_u(1024, 512, 0)
-        turn_l(3)
+        quant_l(1)
+        quant_b(2, 3)
+        mul_l(6)
         finish(512, 0)
-        mul_u(1024, 512, 1)
-        mul_u(1024, 512, 2)
-        finish(0, 1)
-        quant_l(3)
-        mul_u(1024, 512, 3)
-        group_u(1024, 0)
-        finish(512, 1)
+        mul_l(7)
+        turn_l(2)
         finish(0, 2)
+        mul_u(1024, 256, 0)
+        turn_l(3)
+        quant_l(2)
+        mul_u(1024, 256, 1)
         finish(512, 2)
+        mul_u(1024, 256, 2)
+        mul_u(1024, 256, 3)
+        group_u(1024, 0)
+        quant_l(3)
+        finish(0, 4)
+        mul_u(1280, 256, 0)
+        mul_u(1280, 256, 1)
+        finish(512, 4)
+        mul_u(1280, 256, 2)
+        mul_u(1280, 256, 3)
+        group_u(1280, 0)
         quant_u(1024)
-        finish(0, 3)
-        finish(512, 3)
-        for pair in range(PAIRS):
-            finish(1024, pair)
+        finish(0, 6)
+        finish(512, 6)
+        finish(1024, 0)
+        quant_u(1280)
+        finish(1024, 4)
+        finish(1280, 0)
+        finish(1280, 4)

@@ -30,11 +30,11 @@ def tile_row_scaled_schur_update_s12_kernel(tc, c_words, c_scales, f_words, f_sc
     nc = tc.nc
     with ExitStack() as ctx:
         sb = ctx.enter_context(tc.tile_pool(name="sb", bufs=1))
-        psum = ctx.enter_context(tc.psum_pool(name="psum", bufs=8))
+        psum = ctx.enter_context(tc.psum_pool(name="psum", bufs=4))
         ctx.enter_context(tc.manual_schedule())
 
-        def bank(name):
-            return psum.tile([P, WIDE], F32, name=name, tag="bank")
+        def bank(name, side):
+            return psum.tile([P, WIDE], F32, name=name, tag=side)
 
         def stage(name, shape, dtype):
             return sb.tile(shape, dtype, name=name, tag="stage", bufs=STAGE_BUFS, align_bytes=64)
@@ -107,18 +107,17 @@ def tile_row_scaled_schur_update_s12_kernel(tc, c_words, c_scales, f_words, f_sc
         def load_f():
             f_tiles[0] = load_words("f_tile", f_words, 0, 2 * R)
 
-        def load_planes():
-            load_plane(f_plane, f_scales)
-            load_plane(c_plane, c_scales)
 
         for s in range(PACK):
             load_b(0, s)
             load_h(s)
-        for g in range(PASSES):
+        for g in range(3):
             load_b(1, g)
+        load_plane(c_plane, c_scales)
+        load_b(1, 3)
+        load_plane(f_plane, f_scales)
         load_f()
         load_c(0)
-        load_planes()
         load_b(2, 0)
         load_b(2, 1)
         load_c(1)
@@ -130,7 +129,7 @@ def tile_row_scaled_schur_update_s12_kernel(tc, c_words, c_scales, f_words, f_sc
         d_cols = sb.tile([P, PACK], F32, name="d_cols")
         nc.scalar.activation(out=d_cols[:], in_=d_raw[:], func=COPY)
         nc.scalar.copy(out=r_square[0:M_TILES, :], in_=r_rows[:])
-        r_bank = bank("r_bank")
+        r_bank = bank("r_bank", "right")
         nc.tensor.transpose(out=r_bank[:, 0:P], in_=r_square[:], identity=ident[:])
         r_cols = sb.tile([P, M_TILES], F32, name="r_cols")
         nc.scalar.copy(out=r_cols[:], in_=r_bank[:, 0:M_TILES])
@@ -148,7 +147,7 @@ def tile_row_scaled_schur_update_s12_kernel(tc, c_words, c_scales, f_words, f_sc
             words = h_rows[t][:].bitcast(F32)
             h_grouped[t] = sb.tile([P, K], BF16, name="h_grouped%d" % t, tag="grouped", bufs=5, align_bytes=64)
             for half in range(2):
-                turned = bank("h_turned%d_%d" % (t, half))
+                turned = bank("h_turned%d_%d" % (t, half), "right")
                 for i in range(2):
                     g = 2 * half + i
                     for u in range(2):
@@ -166,7 +165,7 @@ def tile_row_scaled_schur_update_s12_kernel(tc, c_words, c_scales, f_words, f_sc
             h_mx[t] = quantize("h%d" % t, h_grouped[t])
 
         def mul_l(j):
-            acc = bank("l_acc%d" % j)
+            acc = bank("l_acc%d" % j, "left")
             c_tile = c_tiles[j // 4]
             first = (j % 4) * 2 * P
             for g in range(PASSES):
@@ -179,7 +178,7 @@ def tile_row_scaled_schur_update_s12_kernel(tc, c_words, c_scales, f_words, f_sc
                     start=(g == 0),
                     stop=(g == PASSES - 1),
                 )
-            l_sorted[j] = sb.tile([P, R], BF16, name="l_sorted%d" % j, tag="l_sorted", bufs=4)
+            l_sorted[j] = sb.tile([P, R], BF16, name="l_sorted%d" % j, tag="l_sorted", bufs=6)
             nc.scalar.activation(
                 out=l_sorted[j][:].rearrange("m (u p e) -> m u p e", u=2, e=2),
                 in_=acc[:].rearrange("m (p u e) -> m u p e", u=2, e=2),
@@ -188,7 +187,7 @@ def tile_row_scaled_schur_update_s12_kernel(tc, c_words, c_scales, f_words, f_sc
             )
 
         def turn_l(pair):
-            turned = bank("l_turned%d" % pair)
+            turned = bank("l_turned%d" % pair, "left")
             for i in range(2):
                 words = l_sorted[2 * pair + i][:].bitcast(F32)
                 for u in range(2):
@@ -209,7 +208,7 @@ def tile_row_scaled_schur_update_s12_kernel(tc, c_words, c_scales, f_words, f_sc
         def pass_u(first, width, t, g):
             chunk, inside = divmod(first, WIDE)
             if g == 0:
-                u_acc[first, t] = bank("u_acc%d_%d" % (first, t))
+                u_acc[first, t] = bank("u_acc%d_%d" % (first, t), "right" if chunk == 1 else "left")
             h_codes, h_scales = h_mx[t]
             b_codes, b_scales = b_mx[chunk, g]
             nc.tensor.matmul_mx(
@@ -245,7 +244,7 @@ def tile_row_scaled_schur_update_s12_kernel(tc, c_words, c_scales, f_words, f_sc
             for i0 in range(0, 2 * per_bank, per_bank):
                 pair, inside = divmod(tile0 + i0, 2)
                 l_codes, l_scales = l_mx[pair]
-                acc = bank("prod%d_%d" % (first, tile0 + i0))
+                acc = bank("prod%d_%d" % (first, tile0 + i0), "right")
                 for i in range(per_bank):
                     rows = slice((inside + i) * P, (inside + i + 1) * P)
                     nc.tensor.matmul_mx(
@@ -265,7 +264,7 @@ def tile_row_scaled_schur_update_s12_kernel(tc, c_words, c_scales, f_words, f_sc
                 )
             nc.sync.dma_start(out=out.rearrange("(j p) n -> p j n", p=P)[:, tile0 : tile0 + 2 * per_bank, cols], in_=result[:])
 
-        group_b(0, 0, 256)
+        group_b(0, 0, 384)
         turn_h(0)
         quant_b(0, 0)
         for s in range(PACK):
@@ -275,23 +274,23 @@ def tile_row_scaled_schur_update_s12_kernel(tc, c_words, c_scales, f_words, f_sc
                 turn_h(s + 1)
                 quant_b(0, s + 1)
             else:
-                group_b(1, 0, 512)
-                group_b(1, 1, 0)
+                group_b(1, 0, 384)
                 quant_h(s)
+                group_b(1, 1, 384)
                 quant_b(1, 0)
-                group_b(1, 2, 512)
+                group_b(1, 2, 384)
             for t in range(s):
                 pass_u(0, 512, t, s)
             for g in range(s + 1):
                 pass_u(0, 512, s, g)
         quant_b(1, 1)
         quant_b(1, 2)
-        group_b(1, 3, 512)
-        group_u(0, 0)
+        group_b(1, 3, 384)
         quant_b(1, 3)
         for g in range(PASSES):
             for t in range(PACK):
                 pass_u(512, 512, t, g)
+        group_u(0, 512)
         quant_u(0)
         group_b(2, 0, 512)
         mul_l(0)
@@ -317,9 +316,9 @@ def tile_row_scaled_schur_update_s12_kernel(tc, c_words, c_scales, f_words, f_sc
         mul_l(6)
         finish(512, 0)
         mul_l(7)
-        turn_l(2)
         finish(0, 2)
         mul_u(1024, 256, 0)
+        turn_l(2)
         turn_l(3)
         quant_l(2)
         mul_u(1024, 256, 1)
@@ -330,13 +329,13 @@ def tile_row_scaled_schur_update_s12_kernel(tc, c_words, c_scales, f_words, f_sc
         quant_l(3)
         finish(0, 4)
         mul_u(1280, 256, 0)
-        mul_u(1280, 256, 1)
         finish(512, 4)
+        mul_u(1280, 256, 1)
+        finish(0, 6)
         mul_u(1280, 256, 2)
         mul_u(1280, 256, 3)
         group_u(1280, 0)
         quant_u(1024)
-        finish(0, 6)
         finish(512, 6)
         finish(1024, 0)
         quant_u(1280)

@@ -17,13 +17,21 @@ COPY = mybir.ActivationFunctionType.Copy
 SUBTRACT = mybir.AluOpType.subtract
 
 P = 128
-PACK = 4
-PASSES = K // (P * PACK)
+SLOTS = 4
+PASSES = K // (P * SLOTS)
 WIDE = 512
-CHUNKS = N // WIDE
-M_TILES = M // P
-PAIRS = M_TILES // 2
+NARROW = WIDE // 2
+ROW_TILES = M // P
+PAIRS = ROW_TILES // 2
+HALF_TILES = ROW_TILES // 2
+NEAR = 4
+
+MOST = 384
+EVEN = 256
+
 STAGE_BUFS = 20
+GROUPED_BUFS = 5
+SORTED_BUFS = 6
 
 
 def tile_row_scaled_schur_update_s12_kernel(tc, c_words, c_scales, f_words, f_scales, h, b, d, r, a, out):
@@ -39,41 +47,52 @@ def tile_row_scaled_schur_update_s12_kernel(tc, c_words, c_scales, f_words, f_sc
         def stage(name, shape, dtype):
             return sb.tile(shape, dtype, name=name, tag="stage", bufs=STAGE_BUFS, align_bytes=64)
 
+        def grouped_tile(name, columns):
+            return sb.tile([P, SLOTS * columns], BF16, name=name, tag="grouped", bufs=GROUPED_BUFS, align_bytes=64)
+
         def quantize(name, grouped):
-            words = grouped.shape[1] // PACK
-            codes = sb.tile([P, words], U32, name=name + "_codes", align_bytes=64)
-            scales = sb.tile([P, words], U8, name=name + "_scales", align_bytes=64)
+            columns = grouped.shape[1] // SLOTS
+            codes = sb.tile([P, columns], U32, name=name + "_codes", align_bytes=64)
+            scales = sb.tile([P, columns], U8, name=name + "_scales", align_bytes=64)
             nc.vector.quantize_mx(out=codes[:].bitcast(FP8X4), scales=scales[:], in_=grouped[:])
             return codes, scales
 
-        def interleave(name, rows, vector_cols):
-            width = rows.shape[2]
-            grouped = sb.tile([P, PACK * width], BF16, name=name, tag="grouped", bufs=5, align_bytes=64)
-            dst = grouped[:].rearrange("p (c i t) -> p c t i", i=4, t=PACK)
-            src = rows[:].rearrange("p t (c i) -> p c t i", i=4)
-            cut = vector_cols // 4
-            if cut < width // 4:
+        def side_by_side(name, rows, vector_cols):
+            columns = rows.shape[2]
+            grouped = grouped_tile(name, columns)
+            dst = grouped[:].rearrange("p (c i t) -> p c t i", i=NEAR, t=SLOTS)
+            src = rows[:].rearrange("p t (c i) -> p c t i", i=NEAR)
+            cut = vector_cols // NEAR
+            if vector_cols < columns:
                 nc.scalar.copy(out=dst[:, cut:], in_=src[:, cut:])
-            if cut > 0:
+            if vector_cols > 0:
                 nc.vector.tensor_copy(out=dst[:, :cut], in_=src[:, :cut])
             return grouped
+
+        def pair_words(grouped_words, turned):
+            nc.scalar.copy(
+                out=grouped_words.rearrange("p (i c u) -> p i c u", i=2, u=2),
+                in_=turned[:].rearrange("p (i u c) -> p i c u", i=2, u=2),
+            )
 
         c_plane = sb.tile([P, PASSES * M], U8, name="c_plane", align_bytes=64)
         f_plane = sb.tile([P, PASSES * R], U8, name="f_plane", align_bytes=64)
         nc.vector.memset(f_plane[:].bitcast(I32), 0)
         nc.vector.memset(c_plane[:].bitcast(I32), 0)
-        d_raw = sb.tile([P, PACK], BF16, name="d_raw")
-        nc.scalar.dma_start(out=d_raw[:], in_=d.rearrange("(p t) -> p t", t=PACK))
-        r_rows = sb.tile([M_TILES, P], BF16, name="r_rows")
+        d_raw = sb.tile([P, SLOTS], BF16, name="d_raw")
+        nc.scalar.dma_start(out=d_raw[:], in_=d.rearrange("(p t) -> p t", t=SLOTS))
+        r_rows = sb.tile([ROW_TILES, P], BF16, name="r_rows")
         nc.scalar.dma_start(out=r_rows[:], in_=r.rearrange("(j p) -> j p", p=P))
         ident = sb.tile([P, P], F32, name="ident")
         make_identity(nc, ident[:])
         r_square = sb.tile([P, P], F32, name="r_square")
         nc.gpsimd.memset(r_square[:], 0.0)
 
-        def load_words(name, words, first, width):
+        h_rows, b_rows, a_rows = {}, {}, {}
+
+        def load_words(name, words, first_byte, width):
             tile = sb.tile([P, PASSES, width], U8, name=name, align_bytes=64)
-            src = words.rearrange("g p w -> p g w")[:, :, first : first + width]
+            src = words.rearrange("g p w -> p g w")[:, :, first_byte : first_byte + width]
             nc.sync.dma_start(out=tile[:].bitcast(I32), in_=src.bitcast(I32))
             return tile
 
@@ -84,68 +103,57 @@ def tile_row_scaled_schur_update_s12_kernel(tc, c_words, c_scales, f_words, f_sc
                     in_=scales.bitcast(I32)[:, row:16:4, :].rearrange("g q w -> q g w"),
                 )
 
-        h_rows, b_rows, a_rows = {}, {}, {}
-
         def load_h(t):
             h_rows[t] = stage("h_rows%d" % t, [P, K], BF16)
-            nc.sync.dma_start(out=h_rows[t][:], in_=h.rearrange("(p t) k -> p t k", t=PACK)[:, t, :])
+            nc.sync.dma_start(out=h_rows[t][:], in_=h.rearrange("(p t) k -> p t k", t=SLOTS)[:, t, :])
 
         def load_b(chunk, g):
-            b_rows[chunk, g] = stage("b_rows%d_%d" % (chunk, g), [P, PACK, WIDE], BF16)
-            src = b[g * P * PACK : (g + 1) * P * PACK, chunk * WIDE : (chunk + 1) * WIDE]
-            nc.sync.dma_start(out=b_rows[chunk, g][:], in_=src.rearrange("(p t) n -> p t n", t=PACK))
+            b_rows[chunk, g] = stage("b_rows%d_%d" % (chunk, g), [P, SLOTS, WIDE], BF16)
+            src = b[g * P * SLOTS : (g + 1) * P * SLOTS, chunk * WIDE : (chunk + 1) * WIDE]
+            nc.sync.dma_start(out=b_rows[chunk, g][:], in_=src.rearrange("(p t) n -> p t n", t=SLOTS))
 
         def load_a(pair):
             a_rows[pair] = sb.tile([P, 2, N], BF16, name="a_rows%d" % pair)
             nc.sync.dma_start(out=a_rows[pair][:], in_=a.rearrange("(j p) n -> p j n", p=P)[:, 2 * pair : 2 * pair + 2, :])
 
-        c_tiles, f_tiles = {}, {}
-
-        def load_c(half):
-            c_tiles[half] = load_words("c_tile%d" % half, c_words, half * M, M)
-
-        def load_f():
-            f_tiles[0] = load_words("f_tile", f_words, 0, 2 * R)
-
-
-        for s in range(PACK):
+        for s in range(SLOTS):
             load_b(0, s)
             load_h(s)
-        for g in range(3):
+        for g in range(PASSES):
             load_b(1, g)
         load_plane(c_plane, c_scales)
-        load_b(1, 3)
+        f_tile = load_words("f_tile", f_words, 0, 2 * R)
         load_plane(f_plane, f_scales)
-        load_f()
-        load_c(0)
+        c_tiles = [load_words("c_tile0", c_words, 0, M)]
         load_b(2, 0)
         load_b(2, 1)
-        load_c(1)
+        c_tiles.append(load_words("c_tile1", c_words, M, M))
         load_b(2, 2)
         load_b(2, 3)
         for pair in range(PAIRS):
             load_a(pair)
 
-        d_cols = sb.tile([P, PACK], F32, name="d_cols")
+        d_cols = sb.tile([P, SLOTS], F32, name="d_cols")
         nc.scalar.activation(out=d_cols[:], in_=d_raw[:], func=COPY)
-        nc.scalar.copy(out=r_square[0:M_TILES, :], in_=r_rows[:])
+        nc.scalar.copy(out=r_square[0:ROW_TILES, :], in_=r_rows[:])
         r_bank = bank("r_bank", "right")
         nc.tensor.transpose(out=r_bank[:, 0:P], in_=r_square[:], identity=ident[:])
-        r_cols = sb.tile([P, M_TILES], F32, name="r_cols")
-        nc.scalar.copy(out=r_cols[:], in_=r_bank[:, 0:M_TILES])
+        r_cols = sb.tile([P, ROW_TILES], F32, name="r_cols")
+        nc.scalar.copy(out=r_cols[:], in_=r_bank[:, 0:ROW_TILES])
 
-        b_grouped, b_mx, h_grouped, h_mx, l_sorted, l_grouped, l_mx = {}, {}, {}, {}, {}, {}, {}
+        b_grouped, b_mx, h_grouped, h_mx = {}, {}, {}, {}
+        l_sorted, l_grouped, l_mx = {}, {}, {}
         u_acc, u_rows, u_grouped, u_mx = {}, {}, {}, {}
 
         def group_b(chunk, g, vector_cols):
-            b_grouped[chunk, g] = interleave("b_grouped%d_%d" % (chunk, g), b_rows[chunk, g], vector_cols)
+            b_grouped[chunk, g] = side_by_side("b_grouped%d_%d" % (chunk, g), b_rows[chunk, g], vector_cols)
 
         def quant_b(chunk, g):
             b_mx[chunk, g] = quantize("b%d_%d" % (chunk, g), b_grouped[chunk, g])
 
         def turn_h(t):
             words = h_rows[t][:].bitcast(F32)
-            h_grouped[t] = sb.tile([P, K], BF16, name="h_grouped%d" % t, tag="grouped", bufs=5, align_bytes=64)
+            h_grouped[t] = grouped_tile("h_grouped%d" % t, PASSES * P)
             for half in range(2):
                 turned = bank("h_turned%d_%d" % (t, half), "right")
                 for i in range(2):
@@ -153,32 +161,28 @@ def tile_row_scaled_schur_update_s12_kernel(tc, c_words, c_scales, f_words, f_sc
                     for u in range(2):
                         nc.tensor.transpose(
                             out=turned[:, (2 * i + u) * P : (2 * i + u + 1) * P],
-                            in_=words[:, 256 * g + u : 256 * (g + 1) : 2],
+                            in_=words[:, 2 * P * g + u : 2 * P * (g + 1) : 2],
                             identity=ident[:],
                         )
-                nc.scalar.copy(
-                    out=h_grouped[t][:].bitcast(F32)[:, half * WIDE : (half + 1) * WIDE].rearrange("p (i c u) -> p i c u", i=2, u=2),
-                    in_=turned[:].rearrange("p (i u c) -> p i c u", i=2, u=2),
-                )
+                pair_words(h_grouped[t][:].bitcast(F32)[:, half * WIDE : (half + 1) * WIDE], turned)
 
         def quant_h(t):
             h_mx[t] = quantize("h%d" % t, h_grouped[t])
 
         def mul_l(j):
             acc = bank("l_acc%d" % j, "left")
-            c_tile = c_tiles[j // 4]
-            first = (j % 4) * 2 * P
+            half, inside = divmod(j, HALF_TILES)
             for g in range(PASSES):
                 nc.tensor.matmul_mx(
                     out=acc[:],
-                    lhsT=c_tile[:, g, first : first + 2 * P].bitcast(FP4X4),
+                    lhsT=c_tiles[half][:, g, 2 * P * inside : 2 * P * (inside + 1)].bitcast(FP4X4),
                     lhsT_scale=c_plane[:, g * M + j * P : g * M + (j + 1) * P],
-                    rhs=f_tiles[0][:, g, :].bitcast(FP4X4),
+                    rhs=f_tile[:, g, :].bitcast(FP4X4),
                     rhs_scale=f_plane[:, g * R : (g + 1) * R],
                     start=(g == 0),
                     stop=(g == PASSES - 1),
                 )
-            l_sorted[j] = sb.tile([P, R], BF16, name="l_sorted%d" % j, tag="l_sorted", bufs=6)
+            l_sorted[j] = sb.tile([P, R], BF16, name="l_sorted%d" % j, tag="l_sorted", bufs=SORTED_BUFS)
             nc.scalar.activation(
                 out=l_sorted[j][:].rearrange("m (u p e) -> m u p e", u=2, e=2),
                 in_=acc[:].rearrange("m (p u e) -> m u p e", u=2, e=2),
@@ -196,19 +200,16 @@ def tile_row_scaled_schur_update_s12_kernel(tc, c_words, c_scales, f_words, f_sc
                         in_=words[:, u * P : (u + 1) * P],
                         identity=ident[:],
                     )
-            l_grouped[pair] = sb.tile([P, 2 * P * PACK], BF16, name="l_grouped%d" % pair, tag="l_grouped", bufs=2, align_bytes=64)
-            nc.scalar.copy(
-                out=l_grouped[pair][:].bitcast(F32).rearrange("p (i c u) -> p i c u", i=2, u=2),
-                in_=turned[:].rearrange("p (i u c) -> p i c u", i=2, u=2),
-            )
+            l_grouped[pair] = sb.tile([P, SLOTS * 2 * P], BF16, name="l_grouped%d" % pair, tag="l_grouped", bufs=2, align_bytes=64)
+            pair_words(l_grouped[pair][:].bitcast(F32), turned)
 
         def quant_l(pair):
             l_mx[pair] = quantize("l%d" % pair, l_grouped[pair])
 
-        def pass_u(first, width, t, g):
+        def pass_u(first, width, side, t, g):
             chunk, inside = divmod(first, WIDE)
             if g == 0:
-                u_acc[first, t] = bank("u_acc%d_%d" % (first, t), "right" if chunk == 1 else "left")
+                u_acc[first, t] = bank("u_acc%d_%d" % (first, t), side)
             h_codes, h_scales = h_mx[t]
             b_codes, b_scales = b_mx[chunk, g]
             nc.tensor.matmul_mx(
@@ -222,15 +223,21 @@ def tile_row_scaled_schur_update_s12_kernel(tc, c_words, c_scales, f_words, f_sc
             )
             if g == PASSES - 1:
                 if t == 0:
-                    u_rows[first] = stage("u_rows%d" % first, [P, PACK, width], BF16)
+                    u_rows[first] = stage("u_rows%d" % first, [P, SLOTS, width], BF16)
                 nc.scalar.activation(out=u_rows[first][:, t, :], in_=u_acc[first, t][:, 0:width], func=COPY, scale=d_cols[:, t : t + 1])
 
-        def mul_u(first, width, t):
+        def new_passes_u0(s):
+            for t in range(s):
+                pass_u(0, WIDE, "left", t, s)
+            for g in range(s + 1):
+                pass_u(0, WIDE, "left", s, g)
+
+        def mul_u_narrow(first, t):
             for g in range(PASSES):
-                pass_u(first, width, t, g)
+                pass_u(first, NARROW, "left", t, g)
 
         def group_u(first, vector_cols):
-            u_grouped[first] = interleave("u_grouped%d" % first, u_rows[first], vector_cols)
+            u_grouped[first] = side_by_side("u_grouped%d" % first, u_rows[first], vector_cols)
 
         def quant_u(first):
             u_mx[first] = quantize("u%d" % first, u_grouped[first])
@@ -264,81 +271,82 @@ def tile_row_scaled_schur_update_s12_kernel(tc, c_words, c_scales, f_words, f_sc
                 )
             nc.sync.dma_start(out=out.rearrange("(j p) n -> p j n", p=P)[:, tile0 : tile0 + 2 * per_bank, cols], in_=result[:])
 
-        group_b(0, 0, 384)
+        u0, u1, u2, u3 = 0, WIDE, 2 * WIDE, 2 * WIDE + NARROW
+
+        group_b(0, 0, MOST)
         turn_h(0)
         quant_b(0, 0)
-        for s in range(PACK):
-            if s < 3:
-                group_b(0, s + 1, 384)
-                quant_h(s)
-                turn_h(s + 1)
-                quant_b(0, s + 1)
-            else:
-                group_b(1, 0, 384)
-                quant_h(s)
-                group_b(1, 1, 384)
-                quant_b(1, 0)
-                group_b(1, 2, 384)
-            for t in range(s):
-                pass_u(0, 512, t, s)
-            for g in range(s + 1):
-                pass_u(0, 512, s, g)
+        for s in range(SLOTS - 1):
+            group_b(0, s + 1, MOST)
+            quant_h(s)
+            turn_h(s + 1)
+            quant_b(0, s + 1)
+            new_passes_u0(s)
+
+        group_b(1, 0, MOST)
+        quant_h(SLOTS - 1)
+        quant_b(1, 0)
+        group_b(1, 1, EVEN)
+        group_b(1, 2, MOST)
         quant_b(1, 1)
+        group_b(1, 3, EVEN)
         quant_b(1, 2)
-        group_b(1, 3, 384)
         quant_b(1, 3)
+        new_passes_u0(SLOTS - 1)
         for g in range(PASSES):
-            for t in range(PACK):
-                pass_u(512, 512, t, g)
-        group_u(0, 512)
-        quant_u(0)
-        group_b(2, 0, 512)
+            for t in range(SLOTS):
+                pass_u(u1, WIDE, "right", t, g)
+
+        group_u(u0, WIDE)
+        quant_u(u0)
+        group_b(2, 0, WIDE)
         mul_l(0)
-        mul_l(1)
-        group_b(2, 1, 512)
         quant_b(2, 0)
-        mul_l(2)
+        group_u(u1, MOST)
+        mul_l(1)
+        group_b(2, 1, MOST)
+        for j in range(2, 5):
+            mul_l(j)
+        quant_u(u1)
         turn_l(0)
-        group_u(512, 384)
-        quant_b(2, 1)
-        mul_l(3)
-        group_b(2, 2, 384)
-        quant_u(512)
-        mul_l(4)
         turn_l(1)
+        group_b(2, 2, WIDE)
+        quant_b(2, 1)
         quant_l(0)
-        group_b(2, 3, 384)
-        quant_b(2, 2)
         mul_l(5)
-        finish(0, 0)
+        group_b(2, 3, MOST)
+        quant_b(2, 2)
         quant_l(1)
-        quant_b(2, 3)
         mul_l(6)
-        finish(512, 0)
+        quant_b(2, 3)
+
+        finish(u0, 0)
         mul_l(7)
-        finish(0, 2)
-        mul_u(1024, 256, 0)
+        finish(u1, 0)
+        mul_u_narrow(u2, 0)
         turn_l(2)
         turn_l(3)
+        mul_u_narrow(u2, 1)
         quant_l(2)
-        mul_u(1024, 256, 1)
-        finish(512, 2)
-        mul_u(1024, 256, 2)
-        mul_u(1024, 256, 3)
-        group_u(1024, 0)
+        finish(u0, 2)
+        mul_u_narrow(u2, 2)
+        finish(u1, 2)
+        mul_u_narrow(u2, 3)
         quant_l(3)
-        finish(0, 4)
-        mul_u(1280, 256, 0)
-        finish(512, 4)
-        mul_u(1280, 256, 1)
-        finish(0, 6)
-        mul_u(1280, 256, 2)
-        mul_u(1280, 256, 3)
-        group_u(1280, 0)
-        quant_u(1024)
-        finish(512, 6)
-        finish(1024, 0)
-        quant_u(1280)
-        finish(1024, 4)
-        finish(1280, 0)
-        finish(1280, 4)
+        finish(u0, 4)
+        group_u(u2, 0)
+        mul_u_narrow(u3, 0)
+        finish(u1, 4)
+        quant_u(u2)
+        mul_u_narrow(u3, 1)
+        mul_u_narrow(u3, 2)
+        finish(u0, 6)
+        mul_u_narrow(u3, 3)
+        group_u(u3, 0)
+
+        finish(u1, 6)
+        finish(u2, 0)
+        quant_u(u3)
+        finish(u2, HALF_TILES)
+        finish(u3, 0)
+        finish(u3, HALF_TILES)

from contextlib import ExitStack

import concourse.mybir as mybir
from concourse.masks import make_identity

M, K, R, N = 1024, 2048, 512, 1536
FLOPS = 2 * M * K * R + 2 * R * K * N + 2 * M * R * N

F32 = mybir.dt.float32
BF16 = mybir.dt.bfloat16
I32 = mybir.dt.int32
U32 = mybir.dt.uint32
U8 = mybir.dt.uint8
FP8X4 = mybir.dt.float8_e4m3fn_x4
FP4X4 = mybir.dt.float4_e2m1fn_x4
COPY = mybir.ActivationFunctionType.Copy
SUBTRACT = mybir.AluOpType.subtract

P = 128
SLOTS = 4
PASSES = K // (P * SLOTS)
WIDE = 512
NARROW = WIDE // 2
ROW_TILES = M // P
PAIRS = ROW_TILES // 2
HALF_TILES = ROW_TILES // 2
NEAR = 4

MOST = 384
EVEN = 256

STAGE_BUFS = 20
GROUPED_BUFS = 5
SORTED_BUFS = 6


def tile_row_scaled_schur_update_s12_kernel(tc, c_words, c_scales, f_words, f_scales, h, b, d, r, a, out):
    nc = tc.nc
    with ExitStack() as ctx:
        sb = ctx.enter_context(tc.tile_pool(name="sb", bufs=1))
        psum = ctx.enter_context(tc.psum_pool(name="psum", bufs=4))
        ctx.enter_context(tc.manual_schedule())

        def bank(name, side):
            return psum.tile([P, WIDE], F32, name=name, tag=side)

        def stage(name, shape, dtype):
            return sb.tile(shape, dtype, name=name, tag="stage", bufs=STAGE_BUFS, align_bytes=64)

        def grouped_tile(name, columns):
            return sb.tile([P, SLOTS * columns], BF16, name=name, tag="grouped", bufs=GROUPED_BUFS, align_bytes=64)

        def quantize(name, grouped):
            columns = grouped.shape[1] // SLOTS
            codes = sb.tile([P, columns], U32, name=name + "_codes", align_bytes=64)
            scales = sb.tile([P, columns], U8, name=name + "_scales", align_bytes=64)
            nc.vector.quantize_mx(out=codes[:].bitcast(FP8X4), scales=scales[:], in_=grouped[:])
            return codes, scales

        def side_by_side(name, rows, vector_cols):
            columns = rows.shape[2]
            grouped = grouped_tile(name, columns)
            dst = grouped[:].rearrange("p (c i t) -> p c t i", i=NEAR, t=SLOTS)
            src = rows[:].rearrange("p t (c i) -> p c t i", i=NEAR)
            cut = vector_cols // NEAR
            if vector_cols < columns:
                nc.scalar.copy(out=dst[:, cut:], in_=src[:, cut:])
            if vector_cols > 0:
                nc.vector.tensor_copy(out=dst[:, :cut], in_=src[:, :cut])
            return grouped

        def pair_words(grouped_words, turned):
            nc.scalar.copy(
                out=grouped_words.rearrange("p (i c u) -> p i c u", i=2, u=2),
                in_=turned[:].rearrange("p (i u c) -> p i c u", i=2, u=2),
            )

        c_plane = sb.tile([P, PASSES * M], U8, name="c_plane", align_bytes=64)
        f_plane = sb.tile([P, PASSES * R], U8, name="f_plane", align_bytes=64)
        nc.vector.memset(f_plane[:].bitcast(I32), 0)
        nc.vector.memset(c_plane[:].bitcast(I32), 0)
        d_raw = sb.tile([P, SLOTS], BF16, name="d_raw")
        nc.scalar.dma_start(out=d_raw[:], in_=d.rearrange("(p t) -> p t", t=SLOTS))
        r_rows = sb.tile([ROW_TILES, P], BF16, name="r_rows")
        nc.scalar.dma_start(out=r_rows[:], in_=r.rearrange("(j p) -> j p", p=P))
        ident = sb.tile([P, P], F32, name="ident")
        make_identity(nc, ident[:])
        r_square = sb.tile([P, P], F32, name="r_square")
        nc.gpsimd.memset(r_square[:], 0.0)

        h_rows, b_rows, a_rows = {}, {}, {}

        def load_words(name, words, first_byte, width):
            tile = sb.tile([P, PASSES, width], U8, name=name, align_bytes=64)
            src = words.rearrange("g p w -> p g w")[:, :, first_byte : first_byte + width]
            nc.sync.dma_start(out=tile[:].bitcast(I32), in_=src.bitcast(I32))
            return tile

        def load_plane(plane, scales):
            for row in range(4):
                nc.sync.dma_start(
                    out=plane[row:P:32, :].bitcast(I32).rearrange("q (g w) -> q g w", g=PASSES),
                    in_=scales.bitcast(I32)[:, row:16:4, :].rearrange("g q w -> q g w"),
                )

        def load_h(t):
            h_rows[t] = stage("h_rows%d" % t, [P, K], BF16)
            nc.sync.dma_start(out=h_rows[t][:], in_=h.rearrange("(p t) k -> p t k", t=SLOTS)[:, t, :])

        def load_b(chunk, g):
            b_rows[chunk, g] = stage("b_rows%d_%d" % (chunk, g), [P, SLOTS, WIDE], BF16)
            src = b[g * P * SLOTS : (g + 1) * P * SLOTS, chunk * WIDE : (chunk + 1) * WIDE]
            nc.sync.dma_start(out=b_rows[chunk, g][:], in_=src.rearrange("(p t) n -> p t n", t=SLOTS))

        def load_a(pair):
            a_rows[pair] = sb.tile([P, 2, N], BF16, name="a_rows%d" % pair)
            nc.sync.dma_start(out=a_rows[pair][:], in_=a.rearrange("(j p) n -> p j n", p=P)[:, 2 * pair : 2 * pair + 2, :])

        for s in range(SLOTS):
            load_b(0, s)
            load_h(s)
        for g in range(PASSES):
            load_b(1, g)
        load_plane(c_plane, c_scales)
        f_tile = load_words("f_tile", f_words, 0, 2 * R)
        load_plane(f_plane, f_scales)
        c_tiles = [load_words("c_tile0", c_words, 0, M)]
        load_b(2, 0)
        load_b(2, 1)
        c_tiles.append(load_words("c_tile1", c_words, M, M))
        load_b(2, 2)
        load_b(2, 3)
        for pair in range(PAIRS):
            load_a(pair)

        d_cols = sb.tile([P, SLOTS], F32, name="d_cols")
        nc.scalar.activation(out=d_cols[:], in_=d_raw[:], func=COPY)
        nc.scalar.copy(out=r_square[0:ROW_TILES, :], in_=r_rows[:])
        r_bank = bank("r_bank", "right")
        nc.tensor.transpose(out=r_bank[:, 0:P], in_=r_square[:], identity=ident[:])
        r_cols = sb.tile([P, ROW_TILES], F32, name="r_cols")
        nc.scalar.copy(out=r_cols[:], in_=r_bank[:, 0:ROW_TILES])

        b_grouped, b_mx, h_grouped, h_mx = {}, {}, {}, {}
        l_sorted, l_grouped, l_mx = {}, {}, {}
        u_acc, u_rows, u_grouped, u_mx = {}, {}, {}, {}

        def group_b(chunk, g, vector_cols):
            b_grouped[chunk, g] = side_by_side("b_grouped%d_%d" % (chunk, g), b_rows[chunk, g], vector_cols)

        def quant_b(chunk, g):
            b_mx[chunk, g] = quantize("b%d_%d" % (chunk, g), b_grouped[chunk, g])

        def turn_h(t):
            words = h_rows[t][:].bitcast(F32)
            h_grouped[t] = grouped_tile("h_grouped%d" % t, PASSES * P)
            for half in range(2):
                turned = bank("h_turned%d_%d" % (t, half), "right")
                for i in range(2):
                    g = 2 * half + i
                    for u in range(2):
                        nc.tensor.transpose(
                            out=turned[:, (2 * i + u) * P : (2 * i + u + 1) * P],
                            in_=words[:, 2 * P * g + u : 2 * P * (g + 1) : 2],
                            identity=ident[:],
                        )
                pair_words(h_grouped[t][:].bitcast(F32)[:, half * WIDE : (half + 1) * WIDE], turned)

        def quant_h(t):
            h_mx[t] = quantize("h%d" % t, h_grouped[t])

        def mul_l(j):
            acc = bank("l_acc%d" % j, "left")
            half, inside = divmod(j, HALF_TILES)
            for g in range(PASSES):
                nc.tensor.matmul_mx(
                    out=acc[:],
                    lhsT=c_tiles[half][:, g, 2 * P * inside : 2 * P * (inside + 1)].bitcast(FP4X4),
                    lhsT_scale=c_plane[:, g * M + j * P : g * M + (j + 1) * P],
                    rhs=f_tile[:, g, :].bitcast(FP4X4),
                    rhs_scale=f_plane[:, g * R : (g + 1) * R],
                    start=(g == 0),
                    stop=(g == PASSES - 1),
                )
            l_sorted[j] = sb.tile([P, R], BF16, name="l_sorted%d" % j, tag="l_sorted", bufs=SORTED_BUFS)
            nc.scalar.activation(
                out=l_sorted[j][:].rearrange("m (u p e) -> m u p e", u=2, e=2),
                in_=acc[:].rearrange("m (p u e) -> m u p e", u=2, e=2),
                func=COPY,
                scale=r_cols[:, j : j + 1],
            )

        def turn_l(pair):
            turned = bank("l_turned%d" % pair, "left")
            for i in range(2):
                words = l_sorted[2 * pair + i][:].bitcast(F32)
                for u in range(2):
                    nc.tensor.transpose(
                        out=turned[:, (2 * i + u) * P : (2 * i + u + 1) * P],
                        in_=words[:, u * P : (u + 1) * P],
                        identity=ident[:],
                    )
            l_grouped[pair] = sb.tile([P, SLOTS * 2 * P], BF16, name="l_grouped%d" % pair, tag="l_grouped", bufs=2, align_bytes=64)
            pair_words(l_grouped[pair][:].bitcast(F32), turned)

        def quant_l(pair):
            l_mx[pair] = quantize("l%d" % pair, l_grouped[pair])

        def pass_u(first, width, side, t, g):
            chunk, inside = divmod(first, WIDE)
            if g == 0:
                u_acc[first, t] = bank("u_acc%d_%d" % (first, t), side)
            h_codes, h_scales = h_mx[t]
            b_codes, b_scales = b_mx[chunk, g]
            nc.tensor.matmul_mx(
                out=u_acc[first, t][:, 0:width],
                lhsT=h_codes[:, g * P : (g + 1) * P].bitcast(FP8X4),
                lhsT_scale=h_scales[:, g * P : (g + 1) * P],
                rhs=b_codes[:, inside : inside + width].bitcast(FP8X4),
                rhs_scale=b_scales[:, inside : inside + width],
                start=(g == 0),
                stop=(g == PASSES - 1),
            )
            if g == PASSES - 1:
                if t == 0:
                    u_rows[first] = stage("u_rows%d" % first, [P, SLOTS, width], BF16)
                nc.scalar.activation(out=u_rows[first][:, t, :], in_=u_acc[first, t][:, 0:width], func=COPY, scale=d_cols[:, t : t + 1])

        def new_passes_u0(s):
            for t in range(s):
                pass_u(0, WIDE, "left", t, s)
            for g in range(s + 1):
                pass_u(0, WIDE, "left", s, g)

        def mul_u_narrow(first, t):
            for g in range(PASSES):
                pass_u(first, NARROW, "left", t, g)

        def group_u(first, vector_cols):
            u_grouped[first] = side_by_side("u_grouped%d" % first, u_rows[first], vector_cols)

        def quant_u(first):
            u_mx[first] = quantize("u%d" % first, u_grouped[first])

        def finish(first, tile0):
            u_codes, u_scales = u_mx[first]
            width = u_codes.shape[1]
            cols = slice(first, first + width)
            per_bank = WIDE // width
            result = stage("result%d_%d" % (first, tile0), [P, 2 * per_bank, width], F32)
            for i0 in range(0, 2 * per_bank, per_bank):
                pair, inside = divmod(tile0 + i0, 2)
                l_codes, l_scales = l_mx[pair]
                acc = bank("prod%d_%d" % (first, tile0 + i0), "right")
                for i in range(per_bank):
                    rows = slice((inside + i) * P, (inside + i + 1) * P)
                    nc.tensor.matmul_mx(
                        out=acc[:, i * width : (i + 1) * width],
                        lhsT=l_codes[:, rows].bitcast(FP8X4),
                        lhsT_scale=l_scales[:, rows],
                        rhs=u_codes[:].bitcast(FP8X4),
                        rhs_scale=u_scales[:],
                        start=True,
                        stop=True,
                    )
                nc.vector.tensor_tensor(
                    out=result[:, i0 : i0 + per_bank, :],
                    in0=a_rows[pair][:, inside : inside + per_bank, cols],
                    in1=acc[:].rearrange("p (i n) -> p i n", i=per_bank),
                    op=SUBTRACT,
                )
            nc.sync.dma_start(out=out.rearrange("(j p) n -> p j n", p=P)[:, tile0 : tile0 + 2 * per_bank, cols], in_=result[:])

        u0, u1, u2, u3 = 0, WIDE, 2 * WIDE, 2 * WIDE + NARROW

        group_b(0, 0, MOST)
        turn_h(0)
        quant_b(0, 0)
        for s in range(SLOTS - 1):
            group_b(0, s + 1, MOST)
            quant_h(s)
            turn_h(s + 1)
            quant_b(0, s + 1)
            new_passes_u0(s)

        group_b(1, 0, MOST)
        quant_h(SLOTS - 1)
        quant_b(1, 0)
        group_b(1, 1, EVEN)
        group_b(1, 2, MOST)
        quant_b(1, 1)
        group_b(1, 3, EVEN)
        quant_b(1, 2)
        quant_b(1, 3)
        new_passes_u0(SLOTS - 1)
        for g in range(PASSES):
            for t in range(SLOTS):
                pass_u(u1, WIDE, "right", t, g)

        group_u(u0, WIDE)
        quant_u(u0)
        group_b(2, 0, WIDE)
        mul_l(0)
        quant_b(2, 0)
        group_u(u1, MOST)
        mul_l(1)
        group_b(2, 1, MOST)
        for j in range(2, 5):
            mul_l(j)
        quant_u(u1)
        turn_l(0)
        turn_l(1)
        group_b(2, 2, WIDE)
        quant_b(2, 1)
        quant_l(0)
        mul_l(5)
        group_b(2, 3, MOST)
        quant_b(2, 2)
        quant_l(1)
        mul_l(6)
        quant_b(2, 3)

        finish(u0, 0)
        mul_l(7)
        finish(u1, 0)
        mul_u_narrow(u2, 0)
        turn_l(2)
        turn_l(3)
        mul_u_narrow(u2, 1)
        quant_l(2)
        finish(u0, 2)
        mul_u_narrow(u2, 2)
        finish(u1, 2)
        mul_u_narrow(u2, 3)
        quant_l(3)
        finish(u0, 4)
        group_u(u2, 0)
        mul_u_narrow(u3, 0)
        finish(u1, 4)
        quant_u(u2)
        mul_u_narrow(u3, 1)
        mul_u_narrow(u3, 2)
        finish(u0, 6)
        mul_u_narrow(u3, 3)
        group_u(u3, 0)

        finish(u1, 6)
        finish(u2, 0)
        quant_u(u3)
        finish(u2, HALF_TILES)
        finish(u3, 0)
        finish(u3, HALF_TILES)
